import numpy as np
import ml_dtypes


def mxq(x, axis, fmt="e4m3"):
    dtype, down = {"e4m3": (ml_dtypes.float8_e4m3fn, 7), "e5m2": (ml_dtypes.float8_e5m2, 14)}[fmt]
    v = np.moveaxis(np.asarray(x, np.float32).astype(ml_dtypes.bfloat16).astype(np.float64), axis, -1)
    blocks = v.reshape(v.shape[:-1] + (-1, 32))
    amax = np.abs(blocks).max(-1, keepdims=True)
    byte = np.maximum(np.where(amax > 0, np.frexp(amax)[1] - 1 + 127, 0) - down, 1)
    scale = np.exp2(byte - 127.0)
    codes = (blocks / scale).astype(np.float32).astype(dtype).astype(np.float64)
    return np.moveaxis((codes * scale).reshape(v.shape), -1, axis)


WIDE = False


def mx_kscale(k):
    if not WIDE:
        return np.ones(k)
    levels = np.array([10, -10, 5, -5, 0])
    if k % 512:
        return np.exp2(np.random.permutation(np.resize(levels, k // 32))).repeat(32)
    a = np.empty((k // 512, 16))
    for p in range(k // 512):
        a[p, :8] = np.random.permutation(np.resize(levels, 8))
        for g in range(8):
            far = levels[np.abs(levels - a[p, g]) >= 10]
            a[p, g + 8] = far[np.random.randint(len(far))]
    return np.exp2(a.ravel()).repeat(32)


def f64(x):
    return np.asarray(x).astype(np.float64)


def striped(idx):
    return np.tile(idx.reshape(-1, 16).T, (8, 1)).astype(np.uint16)


def unstriped(offs):
    return offs[:16].T.reshape(-1).astype(np.int64)


E2M1 = np.array([0.0, 0.5, 1.0, 1.5, 2.0, 3.0, 4.0, 6.0, -0.0, -0.5, -1.0, -1.5, -2.0, -3.0, -4.0, -6.0])


def pack_weight(w, fmt):
    k, n = w.shape
    w = f64(np.asarray(w, np.float32).astype(ml_dtypes.bfloat16)).reshape(k // 32, 32, n)
    amax = np.abs(w).max(1)
    if fmt == "e4m3":
        byte = np.frexp(amax)[1] - 1 + 127 - 7
    else:
        mant, ex = np.frexp(amax / 6.0)
        byte = np.where(mant > 0.5, ex, ex - 1) + 127
    byte = np.clip(np.where(amax > 0, byte, 1), 1, 254)
    scaled = (w * np.exp2(127.0 - byte)[:, None, :]).reshape(k, n).astype(np.float32)
    by_word = np.ascontiguousarray(scaled.reshape(k // 512, 128, 4, n).transpose(0, 1, 3, 2))
    if fmt == "e4m3":
        words = by_word.astype(ml_dtypes.float8_e4m3fn).view(np.uint8)
    else:
        c = by_word.astype(ml_dtypes.float4_e2m1fn).view(np.uint8) & 0xF
        words = (c[..., 0::2] | (c[..., 1::2] << 4)).reshape(k // 512, 128, 2 * n)
    return np.ascontiguousarray(words), np.ascontiguousarray(byte.astype(np.uint8).reshape(k // 512, 16, n))


def unpack_weight(words, scales, fmt):
    g, _, n = scales.shape
    words = np.ascontiguousarray(words).reshape(g, 128, n, -1)
    if fmt == "e4m3":
        vals = words.view(ml_dtypes.float8_e4m3fn).astype(np.float64)
    else:
        nib = np.empty((g, 128, n, 4), np.uint8)
        nib[..., 0::2] = words & 0xF
        nib[..., 1::2] = words >> 4
        vals = E2M1[nib]
    vals = vals * np.repeat(np.exp2(scales.astype(np.float64) - 127.0), 8, axis=1)[..., None]
    return vals.transpose(0, 1, 3, 2).reshape(g * 512, n)


def gelu(v):
    return 0.5 * v * (1.0 + np.tanh(np.sqrt(2.0 / np.pi) * (v + 0.044715 * v**3)))


K, H, T, S, T2, P, T3, S2 = 1024, 512, 2048, 1024, 2048, 512, 2048, 1024

def setup_inputs():
    n = np.random.standard_normal
    s, u = mx_kscale(K)[:, None], mx_kscale(H)[:, None]
    tab_words, tab_scales = pack_weight(n((K, T)) * s, "e4m3")
    tab2_words, tab2_scales = pack_weight(n((H, T3)) / np.sqrt(H) / u, "e4m3")
    w2_words, w2_scales = pack_weight(n((K, H)) / np.sqrt(K) / s * u.T, "e2m1")
    return {
        "tab_words": tab_words, "tab_scales": tab_scales,
        "tab2_words": tab2_words, "tab2_scales": tab2_scales,
        "offs": striped(np.random.permutation(T)[:S]),
        "offs2": striped(np.random.permutation(T3)[:S2]),
        "offs3": striped(np.random.permutation(T2)[:S]),
        "offs4": striped(np.random.permutation(T2)[:P]),
        "w1": (n((K, H)) / np.sqrt(K) / s * u.T).astype(np.float32),
        "w2_words": w2_words, "w2_scales": w2_scales,
        "w3": (n((H, H)) / np.sqrt(H) / u * u.T).astype(np.float32),
        "gain": np.exp(0.4 * n(H)).astype(np.float32),
        "wgs": np.exp(0.3 * n((128, S))).astype(np.float32),
        "page0": (n((H, T2)) * u).astype(np.float32),
        "tune": np.exp(0.4 * n(H)).astype(np.float32),
        "least": n(S2).astype(np.float32),
    }

def reference(tab_words, tab_scales, tab2_words, tab2_scales, offs, offs2, offs3, offs4,
              w1, w2_words, w2_scales, w3, gain, wgs, page0, tune, least):
    v = unpack_weight(tab_words, tab_scales, "e4m3")[:, unstriped(offs)]
    v2 = unpack_weight(tab2_words, tab2_scales, "e4m3")[:, unstriped(offs2)]
    w2 = unpack_weight(w2_words, w2_scales, "e2m1")
    a = mxq(f64(w1), 0, "e4m3").T @ v
    b = w2.T @ v
    d = np.maximum(a, b)
    y = mxq(f64(w3), 0, "e4m3").T @ mxq(d, 0, "e4m3")
    h = f64(gain)[:, None] * (y + a)
    page = f64(page0).copy()
    page[:, unstriped(offs3)] = np.tile(f64(wgs), (H // 128, 1)) * h
    x = page[:, unstriped(offs4)] * f64(tune)[:, None]
    e = v2.T @ mxq(x, 0, "e4m3")
    return np.maximum(e, f64(least)[:, None])

@@ -1,0 +1,236 @@
+from contextlib import ExitStack
+
+import concourse.mybir as mybir
+
+F32 = mybir.dt.float32
+BF16 = mybir.dt.bfloat16
+I32 = mybir.dt.int32
+U32 = mybir.dt.uint32
+U16 = mybir.dt.uint16
+U8 = mybir.dt.uint8
+FP8X4 = mybir.dt.float8_e4m3fn_x4
+FP4X4 = mybir.dt.float4_e2m1fn_x4
+ALU = mybir.AluOpType
+COPY = mybir.ActivationFunctionType.Copy
+
+K, H, T, S, SLOTS, TUNED, CAND = 1024, 512, 2048, 1024, 2048, 512, 1024
+FLOPS = 2 * (2 * K * H * S + H * H * S + H * CAND * TUNED)
+P = 128
+PACK = 4
+PASSES = K // (P * PACK)
+QUADS = 4
+CHUNK = 128
+SLICE = 256
+N_SLICES = S // SLICE
+HALF = TUNED // 2
+
+
+def tile_list_index_advisor_scores_kernel(
+    tc, tab_words, tab_scales, tab2_words, tab2_scales, offs, offs2, offs3, offs4,
+    w1, w2_words, w2_scales, w3, gain, wgs, page0, tune, least, out,
+):
+    nc = tc.nc
+    with ExitStack() as ctx:
+        keep = ctx.enter_context(tc.tile_pool(name="keep", bufs=1))
+        ring = ctx.enter_context(tc.tile_pool(name="ring", bufs=2))
+        psum = ctx.enter_context(tc.psum_pool(name="psum", bufs=1))
+
+        def held(name, shape, dtype):
+            return keep.tile(shape, dtype, name=name, align_bytes=64)
+
+        idx = held("idx", [P, S // 16], U16)
+        idx2 = held("idx2", [P, CAND // 16], U16)
+        idx3 = held("idx3", [P, S // 16], U16)
+        idx4 = held("idx4", [P, TUNED // 16], U16)
+        tab_w = [held(f"tab_w{a}", [P, T], I32) for a in range(PASSES)]
+        tab_s = held("tab_s", [P, T], U8)
+        tab2_w = held("tab2_w", [P, T], I32)
+        tab2_s = held("tab2_s", [P, T], U8)
+        v_w = [held(f"v_w{a}", [P, S], U32) for a in range(PASSES)]
+        v_s = [held(f"v_s{a}", [P, S], U8) for a in range(PASSES)]
+        v2_w = held("v2_w", [P, CAND], U32)
+        v2_s = held("v2_s", [P, CAND], U8)
+        w2_w = held("w2_w", [P, PASSES, 2 * H], U8)
+        w2_s = held("w2_s", [P, PASSES, H], U8)
+        gain_t = held("gain_t", [P, PACK], F32)
+        tune_t = held("tune_t", [P, PACK], F32)
+        least_t = held("least_t", [P, CAND // P], F32)
+        page = [held(f"page{t}", [P, SLOTS], F32) for t in range(PACK)]
+        wgs_t = [held(f"wgs{s}", [P, PACK, SLICE], F32) for s in range(N_SLICES)]
+        w2_c = held("w2_c", [P, PASSES, 2 * H], U8)
+        w2_p = held("w2_p", [P, PASSES, H], U8)
+
+        nc.gpsimd.memset(tab_s[:].bitcast(I32), 0)
+        nc.vector.memset(w2_s[:].bitcast(I32), 0)
+        nc.vector.memset(tab2_s[:].bitcast(I32), 0)
+        nc.vector.memset(v_s[1][:].bitcast(I32), 0)
+
+        def load_words(tile, words):
+            nc.sync.dma_start(out=tile[:], in_=words.rearrange("p t i -> p (t i)").bitcast(I32))
+
+        def load_weight(name, rows, pieces):
+            width = H // pieces
+            raws = []
+            for c in range(pieces):
+                raw = held(f"{name}_raw{c}", [P, PACK, width], F32)
+                nc.sync.dma_start(out=raw[:], in_=rows.rearrange("(p j) c -> p j c", j=PACK)[:, :, c * width:(c + 1) * width])
+                raws.append(raw)
+            return raws
+
+        def load_wgs(s):
+            rows = wgs.rearrange("(m t) j -> m t j", t=PACK)[:, :, s * SLICE:(s + 1) * SLICE]
+            for q in (0, 2, 1, 3):
+                nc.sync.dma_start(out=wgs_t[s][32 * q:32 * q + 32, :, :], in_=rows)
+
+        def load_page(t):
+            nc.sync.dma_start(out=page[t][:], in_=page0.rearrange("(p t) c -> p t c", t=PACK)[:, t, :])
+
+        nc.sync.dma_start(idx[:], offs)
+        nc.sync.dma_start(idx2[:], offs2)
+        nc.sync.dma_start(out=w2_w[:].bitcast(I32), in_=w2_words.rearrange("a p c -> p a c").bitcast(I32))
+        load_words(tab_w[0], tab_words[0])
+        for q in range(QUADS):
+            nc.gpsimd.dma_start(out=tab_s[32 * q:32 * q + 8, :].bitcast(I32), in_=tab_scales[:, 4 * q:4 * q + 4, :].bitcast(I32))
+        load_words(tab_w[1], tab_words[1])
+        w1_raw0 = load_weight("w1a", w1[0:512, :], 1)
+        for q in range(QUADS):
+            nc.gpsimd.dma_start(out=w2_s[32 * q:32 * q + 4, :, :].bitcast(I32),
+                              in_=w2_scales[:, 4 * q:4 * q + 4, :].rearrange("a r c -> r a c").bitcast(I32))
+        for q in range(QUADS):
+            nc.gpsimd.dma_start(out=tab2_s[32 * q:32 * q + 4, :].bitcast(I32), in_=tab2_scales[0, 4 * q:4 * q + 4, :].bitcast(I32))
+        w1_raw1 = load_weight("w1b", w1[512:1024, :], 2)
+        w3_raw = load_weight("w3", w3, 2)
+        nc.sync.dma_start(idx3[:], offs3)
+        nc.sync.dma_start(out=gain_t[:], in_=gain.rearrange("(p t) -> p t", t=PACK))
+        load_words(tab2_w, tab2_words[0])
+        load_wgs(0)
+        load_page(0)
+        load_page(1)
+        load_page(2)
+        load_page(3)
+        load_wgs(1)
+        load_wgs(2)
+        load_wgs(3)
+        nc.sync.dma_start(idx4[:], offs4)
+        nc.sync.dma_start(out=tune_t[:], in_=tune.rearrange("(p t) -> p t", t=PACK))
+        with nc.allow_non_contiguous_dma(reason="one least score a partition"):
+            nc.sync.dma_start(out=least_t[:], in_=least.rearrange("(c p) -> p c", p=P))
+
+        def quantise_weight(name, raws):
+            grouped = held(f"{name}_g", [P, PACK, P, PACK], BF16)
+            codes = held(f"{name}_c", [P, H], U32)
+            plane = held(f"{name}_s", [P, H], U8)
+            width = P // len(raws)
+            for c, raw in enumerate(raws):
+                nc.scalar.copy(
+                    out=grouped[:, :, c * width:(c + 1) * width, :].rearrange("p t m j -> p m j t"),
+                    in_=raw[:].rearrange("p j (m t) -> p m j t", t=PACK),
+                )
+            nc.vector.quantize_mx(out=codes[:].bitcast(FP8X4), scales=plane[:], in_=grouped[:].rearrange("p t m j -> p (t m j)"))
+            return codes, plane
+
+        for a in range(PASSES):
+            nc.vector.tensor_copy(w2_c[:, a, :].rearrange("p (t m b) -> p t m b", t=PACK, b=2),
+                                  w2_w[:, a, :].rearrange("p (m t b) -> p t m b", t=PACK, b=2))
+        nc.vector.tensor_copy(v_w[0][:], tab_w[0][:].bitcast(U32).indirect(idx[:]))
+        nc.vector.tensor_copy(v_s[0][:], tab_s[:].indirect(idx[:]))
+        for q in range(QUADS):
+            nc.gpsimd.dma_start(out=v_s[1][32 * q:32 * q + 4, :].bitcast(I32), in_=v_s[0][32 * q + 4:32 * q + 8, :].bitcast(I32))
+        nc.vector.tensor_copy(w2_p[:].rearrange("p a (t m) -> p a t m", t=PACK), w2_s[:].rearrange("p a (m t) -> p a t m", t=PACK))
+        nc.vector.tensor_copy(v_w[1][:], tab_w[1][:].bitcast(U32).indirect(idx[:]))
+        nc.vector.tensor_copy(v2_s[:], tab2_s[:].indirect(idx2[:]))
+        w1_q = [quantise_weight("w1a", w1_raw0)]
+        w1_q.append(quantise_weight("w1b", w1_raw1))
+        w3_c, w3_s = quantise_weight("w3", w3_raw)
+
+        def bank(tag, bufs, shape):
+            return psum.tile(shape, F32, name=tag, tag=tag, bufs=bufs)
+
+        def readings(s):
+            cols = slice(s * SLICE, (s + 1) * SLICE)
+            a_sb = held(f"a_sb{s}", [P, PACK, SLICE], F32)
+            for pair in range(2):
+                a_ps = bank("a", 2, [P, 2, SLICE])
+                for i in range(2):
+                    ch = slice((2 * pair + i) * P, (2 * pair + i + 1) * P)
+                    for a in range(PASSES):
+                        nc.tensor.matmul_mx(out=a_ps[:, i, :], lhsT=w1_q[a][0][:, ch].bitcast(FP8X4), lhsT_scale=w1_q[a][1][:, ch],
+                                            rhs=v_w[a][:, cols].bitcast(FP8X4), rhs_scale=v_s[0][4 * a:P, cols],
+                                            start=(a == 0), stop=(a == PASSES - 1))
+                nc.scalar.copy(out=a_sb[:, 2 * pair:2 * pair + 2, :], in_=a_ps[:])
+            d_g = ring.tile([P, SLICE, PACK], BF16, name="d_g", align_bytes=64)
+            for c in range(SLICE // CHUNK):
+                part = slice(s * SLICE + c * CHUNK, s * SLICE + (c + 1) * CHUNK)
+                b_ps = bank("b", 3, [P, PACK, CHUNK])
+                for t in range(PACK):
+                    for a in range(PASSES):
+                        nc.tensor.matmul_mx(out=b_ps[:, t, :], lhsT=w2_c[:, a, 2 * t * P:2 * (t + 1) * P].bitcast(FP4X4),
+                                            lhsT_scale=w2_p[:, a, t * P:(t + 1) * P],
+                                            rhs=v_w[a][:, part].bitcast(FP8X4), rhs_scale=v_s[a][:, part],
+                                            start=(a == 0), stop=(a == PASSES - 1))
+                nc.vector.tensor_tensor(
+                    d_g[:, c * CHUNK:(c + 1) * CHUNK, :].rearrange("p (c i) t -> p c t i", i=4),
+                    b_ps[:].rearrange("p t (c i) -> p c t i", i=4),
+                    a_sb[:, :, c * CHUNK:(c + 1) * CHUNK].rearrange("p t (c i) -> p c t i", i=4), ALU.max)
+            d_c = ring.tile([P, SLICE], U32, name="d_c", align_bytes=64)
+            d_s = ring.tile([P, SLICE], U8, name="d_s", align_bytes=64)
+            nc.vector.quantize_mx(out=d_c[:].bitcast(FP8X4), scales=d_s[:], in_=d_g[:].rearrange("p j t -> p (j t)"))
+            y_banks = []
+            for pair in range(2):
+                y_ps = bank("y", 3, [P, 2, SLICE])
+                for i in range(2):
+                    ch = slice((2 * pair + i) * P, (2 * pair + i + 1) * P)
+                    nc.tensor.matmul_mx(out=y_ps[:, i, :], lhsT=w3_c[:, ch].bitcast(FP8X4), lhsT_scale=w3_s[:, ch],
+                                        rhs=d_c[:].bitcast(FP8X4), rhs_scale=d_s[:], start=True, stop=True)
+                y_banks.append(y_ps)
+            return a_sb, y_banks
+
+        def sums(s, a_sb, y_banks):
+            total = held(f"total{s}", [P, PACK, SLICE], F32)
+            factor = held(f"factor{s}", [P, PACK, SLICE], F32)
+            for t in range(PACK):
+                nc.scalar.activation(factor[:, t, :], wgs_t[s][:, t, :], COPY, scale=gain_t[:, t:t + 1])
+            for pair in range(2):
+                nc.vector.tensor_tensor(total[:, 2 * pair:2 * pair + 2, :], y_banks[pair][:], a_sb[:, 2 * pair:2 * pair + 2, :], ALU.add)
+            return total, factor
+
+        x_g = [held(f"x_g{u}", [P, HALF, PACK], BF16) for u in range(2)]
+
+        def fetch(t, u):
+            picked = held(f"picked{t}_{u}", [P, HALF], F32)
+            nc.vector.tensor_copy(picked[:], page[t][:].indirect(idx4[:, u * (HALF // 16):(u + 1) * (HALF // 16)]))
+            nc.scalar.activation(x_g[u][:, :, t], picked[:], COPY, scale=tune_t[:, t:t + 1])
+
+        stage = readings(0)
+        nc.vector.tensor_copy(v2_w[:], tab2_w[:].bitcast(U32).indirect(idx2[:]))
+        for s in range(N_SLICES):
+            total, factor = sums(s, *stage)
+            if s + 1 < N_SLICES:
+                stage = readings(s + 1)
+            for t in range(PACK):
+                nc.vector.tensor_tensor(page[t][:].indirect(idx3[:, s * (SLICE // 16):(s + 1) * (SLICE // 16)]),
+                                        total[:, t, :], factor[:, t, :], ALU.mult)
+                if s == N_SLICES - 1 and t < PACK - 2:
+                    fetch(t, 0)
+                    fetch(t, 1)
+        for u in range(2):
+            fetch(PACK - 2, u)
+            fetch(PACK - 1, u)
+
+        tags = [("a", 2), ("a", 2), ("b", 3), ("b", 3), ("b", 3), ("y", 3), ("y", 3), ("y", 3)]
+        out_rows = out.rearrange("(c p) j -> p c j", p=P)
+        for u in range(2):
+            x_c = held(f"x_c{u}", [P, HALF], U32)
+            x_s = held(f"x_s{u}", [P, HALF], U8)
+            nc.vector.quantize_mx(out=x_c[:].bitcast(FP8X4), scales=x_s[:], in_=x_g[u][:].rearrange("p j t -> p (j t)"))
+            for pair in range(CAND // P // 2):
+                tag, bufs = tags[u * 4 + pair]
+                e_ps = bank(tag, bufs, [P, 2, HALF])
+                for i in range(2):
+                    cols = slice((2 * pair + i) * P, (2 * pair + i + 1) * P)
+                    nc.tensor.matmul_mx(out=e_ps[:, i, :], lhsT=v2_w[:, cols].bitcast(FP8X4), lhsT_scale=v2_s[:, cols],
+                                        rhs=x_c[:].bitcast(FP8X4), rhs_scale=x_s[:], start=True, stop=True)
+                scores = held(f"scores{u}_{pair}", [P, 2, HALF], F32)
+                nc.vector.tensor_tensor(scores[:], e_ps[:],
+                                        least_t[:, 2 * pair:2 * pair + 2].unsqueeze(2).to_broadcast([P, 2, HALF]), ALU.max)
+                nc.sync.dma_start(out=out_rows[:, 2 * pair:2 * pair + 2, u * HALF:(u + 1) * HALF], in_=scores[:])

@@ -1,6 +1,7 @@
 from contextlib import ExitStack
 
 import concourse.mybir as mybir
+from concourse.masks import make_identity
 
 F32 = mybir.dt.float32
 BF16 = mybir.dt.bfloat16
@@ -43,9 +44,9 @@ def tile_list_index_advisor_scores_kernel(
         idx3 = held("idx3", [P, S // 16], U16)
         idx4 = held("idx4", [P, TUNED // 16], U16)
         tab_w = [held(f"tab_w{a}", [P, T], I32) for a in range(PASSES)]
-        tab_s = held("tab_s", [P, T], U8)
+        tab_s = held("tab_s", [P, PASSES, T], U8)
         tab2_w = held("tab2_w", [P, T], I32)
-        tab2_s = held("tab2_s", [P, T], U8)
+        tab2_s = held("tab2_s", [P, 1, T], U8)
         v_w = [held(f"v_w{a}", [P, S], U32) for a in range(PASSES)]
         v_s = [held(f"v_s{a}", [P, S], U8) for a in range(PASSES)]
         v2_w = held("v2_w", [P, CAND], U32)
@@ -57,13 +58,12 @@ def tile_list_index_advisor_scores_kernel(
         least_t = held("least_t", [P, CAND // P], F32)
         page = [held(f"page{t}", [P, SLOTS], F32) for t in range(PACK)]
         wgs_t = [held(f"wgs{s}", [P, PACK, SLICE], F32) for s in range(N_SLICES)]
-        w2_c = held("w2_c", [P, PASSES, 2 * H], U8)
-        w2_p = held("w2_p", [P, PASSES, H], U8)
+        ident = held("ident", [P, P], F32)
 
-        nc.gpsimd.memset(tab_s[:].bitcast(I32), 0)
+        nc.gpsimd.memset(tab_s[:, 0, :].bitcast(I32), 0)
+        nc.vector.memset(tab_s[:, 1, :].bitcast(I32), 0)
         nc.vector.memset(w2_s[:].bitcast(I32), 0)
         nc.vector.memset(tab2_s[:].bitcast(I32), 0)
-        nc.vector.memset(v_s[1][:].bitcast(I32), 0)
 
         def load_words(tile, words):
             nc.sync.dma_start(out=tile[:], in_=words.rearrange("p t i -> p (t i)").bitcast(I32))
@@ -85,114 +85,103 @@ def tile_list_index_advisor_scores_kernel(
         def load_page(t):
             nc.sync.dma_start(out=page[t][:], in_=page0.rearrange("(p t) c -> p t c", t=PACK)[:, t, :])
 
+        def load_scales(tile, scales):
+            for q in range(QUADS):
+                nc.sync.dma_start(out=tile[32 * q:32 * q + 4, :, :].bitcast(I32),
+                                  in_=scales[:, 4 * q:4 * q + 4, :].rearrange("a r c -> r a c").bitcast(I32))
+
         nc.sync.dma_start(idx[:], offs)
+        load_scales(tab_s, tab_scales)
         nc.sync.dma_start(idx2[:], offs2)
-        nc.sync.dma_start(out=w2_w[:].bitcast(I32), in_=w2_words.rearrange("a p c -> p a c").bitcast(I32))
-        load_words(tab_w[0], tab_words[0])
-        for q in range(QUADS):
-            nc.gpsimd.dma_start(out=tab_s[32 * q:32 * q + 8, :].bitcast(I32), in_=tab_scales[:, 4 * q:4 * q + 4, :].bitcast(I32))
-        load_words(tab_w[1], tab_words[1])
-        w1_raw0 = load_weight("w1a", w1[0:512, :], 1)
-        for q in range(QUADS):
-            nc.gpsimd.dma_start(out=w2_s[32 * q:32 * q + 4, :, :].bitcast(I32),
-                              in_=w2_scales[:, 4 * q:4 * q + 4, :].rearrange("a r c -> r a c").bitcast(I32))
-        for q in range(QUADS):
-            nc.gpsimd.dma_start(out=tab2_s[32 * q:32 * q + 4, :].bitcast(I32), in_=tab2_scales[0, 4 * q:4 * q + 4, :].bitcast(I32))
-        w1_raw1 = load_weight("w1b", w1[512:1024, :], 2)
-        w3_raw = load_weight("w3", w3, 2)
         nc.sync.dma_start(idx3[:], offs3)
+        nc.sync.dma_start(idx4[:], offs4)
+        load_words(tab_w[0], tab_words[0])
+        load_scales(tab2_s, tab2_scales)
+        w1_raw0 = load_weight("w1a", w1[0:512, :], 2)
+        w1_raw1 = load_weight("w1b", w1[512:1024, :], 2)
+        nc.sync.dma_start(out=w2_w[:].bitcast(I32), in_=w2_words.rearrange("a p c -> p a c").bitcast(I32))
+        load_scales(w2_s, w2_scales)
+        load_words(tab_w[1], tab_words[1])
+        w3_raw = load_weight("w3", w3, 2)
         nc.sync.dma_start(out=gain_t[:], in_=gain.rearrange("(p t) -> p t", t=PACK))
-        load_words(tab2_w, tab2_words[0])
         load_wgs(0)
         load_page(0)
+        load_words(tab2_w, tab2_words[0])
         load_page(1)
         load_page(2)
         load_page(3)
         load_wgs(1)
         load_wgs(2)
         load_wgs(3)
-        nc.sync.dma_start(idx4[:], offs4)
         nc.sync.dma_start(out=tune_t[:], in_=tune.rearrange("(p t) -> p t", t=PACK))
         with nc.allow_non_contiguous_dma(reason="one least score a partition"):
             nc.sync.dma_start(out=least_t[:], in_=least.rearrange("(c p) -> p c", p=P))
 
         def quantise_weight(name, raws):
-            grouped = held(f"{name}_g", [P, PACK, P, PACK], BF16)
+            grouped = held(f"{name}_g", [P, H, PACK], BF16)
             codes = held(f"{name}_c", [P, H], U32)
             plane = held(f"{name}_s", [P, H], U8)
-            width = P // len(raws)
+            width = H // len(raws)
             for c, raw in enumerate(raws):
                 nc.scalar.copy(
-                    out=grouped[:, :, c * width:(c + 1) * width, :].rearrange("p t m j -> p m j t"),
-                    in_=raw[:].rearrange("p j (m t) -> p m j t", t=PACK),
+                    out=grouped[:, c * width:(c + 1) * width, :].rearrange("p (c i) j -> p c j i", i=4),
+                    in_=raw[:].rearrange("p j (c i) -> p c j i", i=4),
                 )
-            nc.vector.quantize_mx(out=codes[:].bitcast(FP8X4), scales=plane[:], in_=grouped[:].rearrange("p t m j -> p (t m j)"))
+            nc.vector.quantize_mx(out=codes[:].bitcast(FP8X4), scales=plane[:], in_=grouped[:].rearrange("p c j -> p (c j)"))
             return codes, plane
 
         for a in range(PASSES):
-            nc.vector.tensor_copy(w2_c[:, a, :].rearrange("p (t m b) -> p t m b", t=PACK, b=2),
-                                  w2_w[:, a, :].rearrange("p (m t b) -> p t m b", t=PACK, b=2))
+            nc.vector.tensor_copy(v_s[a][:], tab_s[:, a, :].indirect(idx[:]))
         nc.vector.tensor_copy(v_w[0][:], tab_w[0][:].bitcast(U32).indirect(idx[:]))
-        nc.vector.tensor_copy(v_s[0][:], tab_s[:].indirect(idx[:]))
-        for q in range(QUADS):
-            nc.gpsimd.dma_start(out=v_s[1][32 * q:32 * q + 4, :].bitcast(I32), in_=v_s[0][32 * q + 4:32 * q + 8, :].bitcast(I32))
-        nc.vector.tensor_copy(w2_p[:].rearrange("p a (t m) -> p a t m", t=PACK), w2_s[:].rearrange("p a (m t) -> p a t m", t=PACK))
-        nc.vector.tensor_copy(v_w[1][:], tab_w[1][:].bitcast(U32).indirect(idx[:]))
-        nc.vector.tensor_copy(v2_s[:], tab2_s[:].indirect(idx2[:]))
+        make_identity(nc, ident[:])
         w1_q = [quantise_weight("w1a", w1_raw0)]
+        nc.vector.tensor_copy(v2_s[:], tab2_s[:, 0, :].indirect(idx2[:]))
         w1_q.append(quantise_weight("w1b", w1_raw1))
+        for u in range(2):
+            nc.vector.tensor_copy(v_w[1][:, u * S // 2:(u + 1) * S // 2], tab_w[1][:].bitcast(U32).indirect(idx[:, u * S // 32:(u + 1) * S // 32]))
         w3_c, w3_s = quantise_weight("w3", w3_raw)
 
         def bank(tag, bufs, shape):
             return psum.tile(shape, F32, name=tag, tag=tag, bufs=bufs)
 
-        def readings(s):
-            cols = slice(s * SLICE, (s + 1) * SLICE)
-            a_sb = held(f"a_sb{s}", [P, PACK, SLICE], F32)
-            for pair in range(2):
-                a_ps = bank("a", 2, [P, 2, SLICE])
-                for i in range(2):
-                    ch = slice((2 * pair + i) * P, (2 * pair + i + 1) * P)
-                    for a in range(PASSES):
-                        nc.tensor.matmul_mx(out=a_ps[:, i, :], lhsT=w1_q[a][0][:, ch].bitcast(FP8X4), lhsT_scale=w1_q[a][1][:, ch],
-                                            rhs=v_w[a][:, cols].bitcast(FP8X4), rhs_scale=v_s[0][4 * a:P, cols],
-                                            start=(a == 0), stop=(a == PASSES - 1))
-                nc.scalar.copy(out=a_sb[:, 2 * pair:2 * pair + 2, :], in_=a_ps[:])
-            d_g = ring.tile([P, SLICE, PACK], BF16, name="d_g", align_bytes=64)
-            for c in range(SLICE // CHUNK):
-                part = slice(s * SLICE + c * CHUNK, s * SLICE + (c + 1) * CHUNK)
-                b_ps = bank("b", 3, [P, PACK, CHUNK])
-                for t in range(PACK):
-                    for a in range(PASSES):
-                        nc.tensor.matmul_mx(out=b_ps[:, t, :], lhsT=w2_c[:, a, 2 * t * P:2 * (t + 1) * P].bitcast(FP4X4),
-                                            lhsT_scale=w2_p[:, a, t * P:(t + 1) * P],
-                                            rhs=v_w[a][:, part].bitcast(FP8X4), rhs_scale=v_s[a][:, part],
-                                            start=(a == 0), stop=(a == PASSES - 1))
-                nc.vector.tensor_tensor(
-                    d_g[:, c * CHUNK:(c + 1) * CHUNK, :].rearrange("p (c i) t -> p c t i", i=4),
-                    b_ps[:].rearrange("p t (c i) -> p c t i", i=4),
-                    a_sb[:, :, c * CHUNK:(c + 1) * CHUNK].rearrange("p t (c i) -> p c t i", i=4), ALU.max)
-            d_c = ring.tile([P, SLICE], U32, name="d_c", align_bytes=64)
-            d_s = ring.tile([P, SLICE], U8, name="d_s", align_bytes=64)
-            nc.vector.quantize_mx(out=d_c[:].bitcast(FP8X4), scales=d_s[:], in_=d_g[:].rearrange("p j t -> p (j t)"))
-            y_banks = []
-            for pair in range(2):
-                y_ps = bank("y", 3, [P, 2, SLICE])
-                for i in range(2):
-                    ch = slice((2 * pair + i) * P, (2 * pair + i + 1) * P)
-                    nc.tensor.matmul_mx(out=y_ps[:, i, :], lhsT=w3_c[:, ch].bitcast(FP8X4), lhsT_scale=w3_s[:, ch],
-                                        rhs=d_c[:].bitcast(FP8X4), rhs_scale=d_s[:], start=True, stop=True)
-                y_banks.append(y_ps)
-            return a_sb, y_banks
-
-        def sums(s, a_sb, y_banks):
-            total = held(f"total{s}", [P, PACK, SLICE], F32)
-            factor = held(f"factor{s}", [P, PACK, SLICE], F32)
+        def chunk(c, h_tiles):
+            cols = slice(c * CHUNK, (c + 1) * CHUNK)
+            a_ps = bank("a", 2, [P, H])
+            b_ps = bank("b", 2, [P, H])
+            for a in range(PASSES):
+                nc.tensor.matmul_mx(out=a_ps[:], lhsT=v_w[a][:, cols].bitcast(FP8X4), lhsT_scale=v_s[a][:, cols],
+                                    rhs=w1_q[a][0][:].bitcast(FP8X4), rhs_scale=w1_q[a][1][:],
+                                    start=(a == 0), stop=(a == PASSES - 1))
+            for a in range(PASSES):
+                nc.tensor.matmul_mx(out=b_ps[:], lhsT=v_w[a][:, cols].bitcast(FP8X4), lhsT_scale=v_s[a][:, cols],
+                                    rhs=w2_w[:, a, :].bitcast(FP4X4), rhs_scale=w2_s[:, a, :],
+                                    start=(a == 0), stop=(a == PASSES - 1))
+            a_sb = ring.tile([P, PACK, P], F32, name="a_sb", bufs=3)
+            nc.scalar.copy(out=a_sb[:], in_=a_ps[:].rearrange("p (m t) -> p t m", t=PACK))
+            d_t = ring.tile([P, 2, P, 2], BF16, name="d_t")
+            nc.vector.tensor_tensor(d_t[:], b_ps[:].rearrange("p (m u e) -> p u m e", u=2, e=2),
+                                    a_sb[:].rearrange("p (u e) m -> p u m e", e=2), ALU.max)
+            d_words = d_t[:].rearrange("p u m e -> p (u m e)").bitcast(F32)
+            d_ps = bank("d", 1, [P, 2, CHUNK])
+            for u in range(2):
+                nc.tensor.transpose(d_ps[:, u, :], d_words[:, u * P:(u + 1) * P], ident[:])
+            d_g = ring.tile([P, CHUNK * PACK], BF16, name="d_g", align_bytes=64)
+            nc.scalar.copy(out=d_g[:].bitcast(F32).rearrange("p (j u) -> p j u", u=2), in_=d_ps[:].rearrange("p u j -> p j u"))
+            d_c = ring.tile([P, CHUNK], U32, name="d_c", align_bytes=64)
+            d_s = ring.tile([P, CHUNK], U8, name="d_s", align_bytes=64)
+            nc.vector.quantize_mx(out=d_c[:].bitcast(FP8X4), scales=d_s[:], in_=d_g[:])
+            y_ps = bank("y", 1, [P, H])
+            nc.tensor.matmul_mx(out=y_ps[:], lhsT=d_c[:].bitcast(FP8X4), lhsT_scale=d_s[:],
+                                rhs=w3_c[:].bitcast(FP8X4), rhs_scale=w3_s[:], start=True, stop=True)
+            y_sb = ring.tile([P, PACK, P], F32, name="y_sb")
+            nc.scalar.copy(out=y_sb[:], in_=y_ps[:].rearrange("p (m t) -> p t m", t=PACK))
+            h_ps = bank("h", 2, [P, PACK, CHUNK])
             for t in range(PACK):
-                nc.scalar.activation(factor[:, t, :], wgs_t[s][:, t, :], COPY, scale=gain_t[:, t:t + 1])
-            for pair in range(2):
-                nc.vector.tensor_tensor(total[:, 2 * pair:2 * pair + 2, :], y_banks[pair][:], a_sb[:, 2 * pair:2 * pair + 2, :], ALU.add)
-            return total, factor
+                nc.tensor.matmul(h_ps[:, t, :], lhsT=a_sb[:, t, :], rhs=ident[:], is_transpose=True, start=True, stop=False)
+                nc.tensor.matmul(h_ps[:, t, :], lhsT=y_sb[:, t, :], rhs=ident[:], is_transpose=True, start=False, stop=True)
+            at = (c * CHUNK) % SLICE
+            for t in range(PACK):
+                nc.scalar.activation(h_tiles[t][:, at:at + CHUNK], h_ps[:, t, :], COPY, scale=gain_t[:, t:t + 1])
 
         x_g = [held(f"x_g{u}", [P, HALF, PACK], BF16) for u in range(2)]
 
@@ -201,15 +190,15 @@ def tile_list_index_advisor_scores_kernel(
             nc.vector.tensor_copy(picked[:], page[t][:].indirect(idx4[:, u * (HALF // 16):(u + 1) * (HALF // 16)]))
             nc.scalar.activation(x_g[u][:, :, t], picked[:], COPY, scale=tune_t[:, t:t + 1])
 
-        stage = readings(0)
-        nc.vector.tensor_copy(v2_w[:], tab2_w[:].bitcast(U32).indirect(idx2[:]))
         for s in range(N_SLICES):
-            total, factor = sums(s, *stage)
-            if s + 1 < N_SLICES:
-                stage = readings(s + 1)
+            h_tiles = [held(f"h{s}_{t}", [P, SLICE], F32) for t in range(PACK)]
+            for c in range(s * SLICE // CHUNK, (s + 1) * SLICE // CHUNK):
+                chunk(c, h_tiles)
+            if s == 0:
+                nc.vector.tensor_copy(v2_w[:], tab2_w[:].bitcast(U32).indirect(idx2[:]))
             for t in range(PACK):
                 nc.vector.tensor_tensor(page[t][:].indirect(idx3[:, s * (SLICE // 16):(s + 1) * (SLICE // 16)]),
-                                        total[:, t, :], factor[:, t, :], ALU.mult)
+                                        h_tiles[t][:], wgs_t[s][:, t, :], ALU.mult)
                 if s == N_SLICES - 1 and t < PACK - 2:
                     fetch(t, 0)
                     fetch(t, 1)
@@ -217,7 +206,7 @@ def tile_list_index_advisor_scores_kernel(
             fetch(PACK - 2, u)
             fetch(PACK - 1, u)
 
-        tags = [("a", 2), ("a", 2), ("b", 3), ("b", 3), ("b", 3), ("y", 3), ("y", 3), ("y", 3)]
+        tags = [("a", 2), ("a", 2), ("b", 2), ("b", 2), ("h", 2), ("h", 2), ("d", 1), ("y", 1)]
         out_rows = out.rearrange("(c p) j -> p c j", p=P)
         for u in range(2):
             x_c = held(f"x_c{u}", [P, HALF], U32)

@@ -74,7 +74,7 @@ def tile_list_index_advisor_scores_kernel(
             for c in range(pieces):
                 raw = held(f"{name}_raw{c}", [P, PACK, width], F32)
                 nc.sync.dma_start(out=raw[:], in_=rows.rearrange("(p j) c -> p j c", j=PACK)[:, :, c * width:(c + 1) * width])
-                raws.append(raw)
+                raws.extend(raw[:, :, i:i + H // 2] for i in range(0, width, H // 2))
             return raws
 
         def load_wgs(s):
@@ -86,7 +86,7 @@ def tile_list_index_advisor_scores_kernel(
             nc.sync.dma_start(out=page[t][:], in_=page0.rearrange("(p t) c -> p t c", t=PACK)[:, t, :])
 
         def load_scales(tile, scales):
-            for q in range(QUADS):
+            for q in (0, 2, 1, 3):
                 nc.sync.dma_start(out=tile[32 * q:32 * q + 4, :, :].bitcast(I32),
                                   in_=scales[:, 4 * q:4 * q + 4, :].rearrange("a r c -> r a c").bitcast(I32))
 
@@ -97,12 +97,12 @@ def tile_list_index_advisor_scores_kernel(
         nc.sync.dma_start(idx4[:], offs4)
         load_words(tab_w[0], tab_words[0])
         load_scales(tab2_s, tab2_scales)
-        w1_raw0 = load_weight("w1a", w1[0:512, :], 2)
+        w1_raw0 = load_weight("w1a", w1[0:512, :], 1)
         w1_raw1 = load_weight("w1b", w1[512:1024, :], 2)
         nc.sync.dma_start(out=w2_w[:].bitcast(I32), in_=w2_words.rearrange("a p c -> p a c").bitcast(I32))
         load_scales(w2_s, w2_scales)
         load_words(tab_w[1], tab_words[1])
-        w3_raw = load_weight("w3", w3, 2)
+        w3_raw = load_weight("w3", w3, 1)
         nc.sync.dma_start(out=gain_t[:], in_=gain.rearrange("(p t) -> p t", t=PACK))
         load_wgs(0)
         load_page(0)
@@ -117,16 +117,18 @@ def tile_list_index_advisor_scores_kernel(
         with nc.allow_non_contiguous_dma(reason="one least score a partition"):
             nc.sync.dma_start(out=least_t[:], in_=least.rearrange("(c p) -> p c", p=P))
 
-        def quantise_weight(name, raws):
+        def quantise_weight(name, raws, dealt=False):
             grouped = held(f"{name}_g", [P, H, PACK], BF16)
             codes = held(f"{name}_c", [P, H], U32)
             plane = held(f"{name}_s", [P, H], U8)
             width = H // len(raws)
             for c, raw in enumerate(raws):
-                nc.scalar.copy(
-                    out=grouped[:, c * width:(c + 1) * width, :].rearrange("p (c i) j -> p c j i", i=4),
-                    in_=raw[:].rearrange("p j (c i) -> p c j i", i=4),
-                )
+                if dealt:
+                    rows = slice(c * width // PACK, (c + 1) * width // PACK)
+                    target = grouped[:].rearrange("p (t m) j -> p m j t", t=PACK)[:, rows, :, :]
+                else:
+                    target = grouped[:, c * width:(c + 1) * width, :].rearrange("p (m t) j -> p m j t", t=PACK)
+                nc.scalar.copy(out=target, in_=raw.rearrange("p j (m t) -> p m j t", t=PACK))
             nc.vector.quantize_mx(out=codes[:].bitcast(FP8X4), scales=plane[:], in_=grouped[:].rearrange("p c j -> p (c j)"))
             return codes, plane
 
@@ -139,12 +141,12 @@ def tile_list_index_advisor_scores_kernel(
         w1_q.append(quantise_weight("w1b", w1_raw1))
         for u in range(2):
             nc.vector.tensor_copy(v_w[1][:, u * S // 2:(u + 1) * S // 2], tab_w[1][:].bitcast(U32).indirect(idx[:, u * S // 32:(u + 1) * S // 32]))
-        w3_c, w3_s = quantise_weight("w3", w3_raw)
+        w3_c, w3_s = quantise_weight("w3", w3_raw, True)
 
         def bank(tag, bufs, shape):
             return psum.tile(shape, F32, name=tag, tag=tag, bufs=bufs)
 
-        def chunk(c, h_tiles):
+        def front(c):
             cols = slice(c * CHUNK, (c + 1) * CHUNK)
             a_ps = bank("a", 2, [P, H])
             b_ps = bank("b", 2, [P, H])
@@ -156,7 +158,7 @@ def tile_list_index_advisor_scores_kernel(
                 nc.tensor.matmul_mx(out=b_ps[:], lhsT=v_w[a][:, cols].bitcast(FP8X4), lhsT_scale=v_s[a][:, cols],
                                     rhs=w2_w[:, a, :].bitcast(FP4X4), rhs_scale=w2_s[:, a, :],
                                     start=(a == 0), stop=(a == PASSES - 1))
-            a_sb = ring.tile([P, PACK, P], F32, name="a_sb", bufs=3)
+            a_sb = held(f"a_sb{c}", [P, PACK, P], F32)
             nc.scalar.copy(out=a_sb[:], in_=a_ps[:].rearrange("p (m t) -> p t m", t=PACK))
             d_t = ring.tile([P, 2, P, 2], BF16, name="d_t")
             nc.vector.tensor_tensor(d_t[:], b_ps[:].rearrange("p (m u e) -> p u m e", u=2, e=2),
@@ -167,19 +169,36 @@ def tile_list_index_advisor_scores_kernel(
                 nc.tensor.transpose(d_ps[:, u, :], d_words[:, u * P:(u + 1) * P], ident[:])
             d_g = ring.tile([P, CHUNK * PACK], BF16, name="d_g", align_bytes=64)
             nc.scalar.copy(out=d_g[:].bitcast(F32).rearrange("p (j u) -> p j u", u=2), in_=d_ps[:].rearrange("p u j -> p j u"))
-            d_c = ring.tile([P, CHUNK], U32, name="d_c", align_bytes=64)
-            d_s = ring.tile([P, CHUNK], U8, name="d_s", align_bytes=64)
+            d_c = held(f"d_c{c}", [P, CHUNK], U32)
+            d_s = held(f"d_s{c}", [P, CHUNK], U8)
             nc.vector.quantize_mx(out=d_c[:].bitcast(FP8X4), scales=d_s[:], in_=d_g[:])
+            return a_sb, d_c, d_s
+
+        def back(c, h_tiles, a_sb, d_c, d_s):
+            at = (c * CHUNK) % SLICE
+            h_ps = bank("h", 2, [P, PACK, CHUNK])
+            if c < SLICE // CHUNK:
+                for t in range(PACK):
+                    nc.tensor.transpose(h_ps[:, t, :], a_sb[:, t, :], ident[:])
+                a_gain = ring.tile([P, PACK, CHUNK], F32, name="a_gain")
+                for t in range(PACK):
+                    nc.scalar.activation(a_gain[:, t, :], h_ps[:, t, :], COPY, scale=gain_t[:, t:t + 1])
+                y_ps = bank("y", 1, [P, PACK, CHUNK])
+                for t in range(PACK):
+                    nc.tensor.matmul_mx(out=y_ps[:, t, :], lhsT=w3_c[:, t * P:(t + 1) * P].bitcast(FP8X4), lhsT_scale=w3_s[:, t * P:(t + 1) * P],
+                                        rhs=d_c[:].bitcast(FP8X4), rhs_scale=d_s[:], start=True, stop=True)
+                for t in range(PACK):
+                    nc.vector.scalar_tensor_tensor(h_tiles[t][:, at:at + CHUNK], y_ps[:, t, :], gain_t[:, t:t + 1], a_gain[:, t, :],
+                                                   ALU.mult, ALU.add)
+                return
             y_ps = bank("y", 1, [P, H])
             nc.tensor.matmul_mx(out=y_ps[:], lhsT=d_c[:].bitcast(FP8X4), lhsT_scale=d_s[:],
                                 rhs=w3_c[:].bitcast(FP8X4), rhs_scale=w3_s[:], start=True, stop=True)
-            y_sb = ring.tile([P, PACK, P], F32, name="y_sb")
-            nc.scalar.copy(out=y_sb[:], in_=y_ps[:].rearrange("p (m t) -> p t m", t=PACK))
-            h_ps = bank("h", 2, [P, PACK, CHUNK])
+            y_sb = ring.tile([P, H], F32, name="y_sb")
+            nc.scalar.copy(out=y_sb[:], in_=y_ps[:])
             for t in range(PACK):
                 nc.tensor.matmul(h_ps[:, t, :], lhsT=a_sb[:, t, :], rhs=ident[:], is_transpose=True, start=True, stop=False)
-                nc.tensor.matmul(h_ps[:, t, :], lhsT=y_sb[:, t, :], rhs=ident[:], is_transpose=True, start=False, stop=True)
-            at = (c * CHUNK) % SLICE
+                nc.tensor.matmul(h_ps[:, t, :], lhsT=y_sb[:, t * P:(t + 1) * P], rhs=ident[:], is_transpose=True, start=False, stop=True)
             for t in range(PACK):
                 nc.scalar.activation(h_tiles[t][:, at:at + CHUNK], h_ps[:, t, :], COPY, scale=gain_t[:, t:t + 1])
 
@@ -190,21 +209,38 @@ def tile_list_index_advisor_scores_kernel(
             nc.vector.tensor_copy(picked[:], page[t][:].indirect(idx4[:, u * (HALF // 16):(u + 1) * (HALF // 16)]))
             nc.scalar.activation(x_g[u][:, :, t], picked[:], COPY, scale=tune_t[:, t:t + 1])
 
+        per = SLICE // CHUNK
+        fronts = {}
+        h_all = [[held(f"h{s}_{t}", [P, SLICE], F32) for t in range(PACK)] for s in range(N_SLICES)]
+
+        def fronts_of(s):
+            for c in range(s * per, (s + 1) * per):
+                fronts[c] = front(c)
+
+        def backs_of(s):
+            for c in range(s * per, (s + 1) * per):
+                back(c, h_all[s], *fronts[c])
+
+        fronts_of(0)
+        backs_of(0)
+        fronts_of(1)
+        nc.vector.tensor_copy(v2_w[:], tab2_w[:].bitcast(U32).indirect(idx2[:]))
         for s in range(N_SLICES):
-            h_tiles = [held(f"h{s}_{t}", [P, SLICE], F32) for t in range(PACK)]
-            for c in range(s * SLICE // CHUNK, (s + 1) * SLICE // CHUNK):
-                chunk(c, h_tiles)
-            if s == 0:
-                nc.vector.tensor_copy(v2_w[:], tab2_w[:].bitcast(U32).indirect(idx2[:]))
+            h_tiles = h_all[s]
+            if s + 2 < N_SLICES:
+                fronts_of(s + 2)
             for t in range(PACK):
+                if s == N_SLICES - 1 and t == PACK - 1:
+                    for done in range(1, PACK - 1):
+                        fetch(done, 0)
+                        fetch(done, 1)
                 nc.vector.tensor_tensor(page[t][:].indirect(idx3[:, s * (SLICE // 16):(s + 1) * (SLICE // 16)]),
                                         h_tiles[t][:], wgs_t[s][:, t, :], ALU.mult)
-                if s == N_SLICES - 1 and t < PACK - 2:
+                if s == N_SLICES - 1 and t in (0, PACK - 1):
                     fetch(t, 0)
                     fetch(t, 1)
-        for u in range(2):
-            fetch(PACK - 2, u)
-            fetch(PACK - 1, u)
+            if s + 1 < N_SLICES:
+                backs_of(s + 1)
 
         tags = [("a", 2), ("a", 2), ("b", 2), ("b", 2), ("h", 2), ("h", 2), ("d", 1), ("y", 1)]
         out_rows = out.rearrange("(c p) j -> p c j", p=P)

from contextlib import ExitStack

import concourse.mybir as mybir
from concourse.masks import make_identity

F32 = mybir.dt.float32
BF16 = mybir.dt.bfloat16
I32 = mybir.dt.int32
U32 = mybir.dt.uint32
U16 = mybir.dt.uint16
U8 = mybir.dt.uint8
FP8X4 = mybir.dt.float8_e4m3fn_x4
FP4X4 = mybir.dt.float4_e2m1fn_x4
ALU = mybir.AluOpType
COPY = mybir.ActivationFunctionType.Copy

K, H, T, S, SLOTS, TUNED, CAND = 1024, 512, 2048, 1024, 2048, 512, 1024
FLOPS = 2 * (2 * K * H * S + H * H * S + H * CAND * TUNED)
P = 128
PACK = 4
PASSES = K // (P * PACK)
QUADS = 4
CHUNK = 128
SLICE = 256
N_SLICES = S // SLICE
HALF = TUNED // 2


def tile_list_index_advisor_scores_kernel(
    tc, tab_words, tab_scales, tab2_words, tab2_scales, offs, offs2, offs3, offs4,
    w1, w2_words, w2_scales, w3, gain, wgs, page0, tune, least, out,
):
    nc = tc.nc
    with ExitStack() as ctx:
        keep = ctx.enter_context(tc.tile_pool(name="keep", bufs=1))
        ring = ctx.enter_context(tc.tile_pool(name="ring", bufs=2))
        psum = ctx.enter_context(tc.psum_pool(name="psum", bufs=1))

        def held(name, shape, dtype):
            return keep.tile(shape, dtype, name=name, align_bytes=64)

        idx = held("idx", [P, S // 16], U16)
        idx2 = held("idx2", [P, CAND // 16], U16)
        idx3 = held("idx3", [P, S // 16], U16)
        idx4 = held("idx4", [P, TUNED // 16], U16)
        tab_w = [held(f"tab_w{a}", [P, T], I32) for a in range(PASSES)]
        tab_s = held("tab_s", [P, PASSES, T], U8)
        tab2_w = held("tab2_w", [P, T], I32)
        tab2_s = held("tab2_s", [P, 1, T], U8)
        v_w = [held(f"v_w{a}", [P, S], U32) for a in range(PASSES)]
        v_s = [held(f"v_s{a}", [P, S], U8) for a in range(PASSES)]
        v2_w = held("v2_w", [P, CAND], U32)
        v2_s = held("v2_s", [P, CAND], U8)
        w2_w = held("w2_w", [P, PASSES, 2 * H], U8)
        w2_s = held("w2_s", [P, PASSES, H], U8)
        gain_t = held("gain_t", [P, PACK], F32)
        tune_t = held("tune_t", [P, PACK], F32)
        least_t = held("least_t", [P, CAND // P], F32)
        page = [held(f"page{t}", [P, SLOTS], F32) for t in range(PACK)]
        wgs_t = [held(f"wgs{s}", [P, PACK, SLICE], F32) for s in range(N_SLICES)]
        ident = held("ident", [P, P], F32)

        nc.gpsimd.memset(tab_s[:, 0, :].bitcast(I32), 0)
        nc.vector.memset(tab_s[:, 1, :].bitcast(I32), 0)
        nc.vector.memset(w2_s[:].bitcast(I32), 0)
        nc.vector.memset(tab2_s[:].bitcast(I32), 0)

        def load_words(tile, words):
            nc.sync.dma_start(out=tile[:], in_=words.rearrange("p t i -> p (t i)").bitcast(I32))

        def load_weight(name, rows, pieces):
            width = H // pieces
            raws = []
            for c in range(pieces):
                raw = held(f"{name}_raw{c}", [P, PACK, width], F32)
                nc.sync.dma_start(out=raw[:], in_=rows.rearrange("(p j) c -> p j c", j=PACK)[:, :, c * width:(c + 1) * width])
                raws.extend(raw[:, :, i:i + H // 2] for i in range(0, width, H // 2))
            return raws

        def load_wgs(s):
            rows = wgs.rearrange("(m t) j -> m t j", t=PACK)[:, :, s * SLICE:(s + 1) * SLICE]
            for q in (0, 2, 1, 3):
                nc.sync.dma_start(out=wgs_t[s][32 * q:32 * q + 32, :, :], in_=rows)

        def load_page(t):
            nc.sync.dma_start(out=page[t][:], in_=page0.rearrange("(p t) c -> p t c", t=PACK)[:, t, :])

        def load_scales(tile, scales):
            for q in (0, 2, 1, 3):
                nc.sync.dma_start(out=tile[32 * q:32 * q + 4, :, :].bitcast(I32),
                                  in_=scales[:, 4 * q:4 * q + 4, :].rearrange("a r c -> r a c").bitcast(I32))

        nc.sync.dma_start(idx[:], offs)
        load_scales(tab_s, tab_scales)
        nc.sync.dma_start(idx2[:], offs2)
        nc.sync.dma_start(idx3[:], offs3)
        nc.sync.dma_start(idx4[:], offs4)
        load_words(tab_w[0], tab_words[0])
        load_scales(tab2_s, tab2_scales)
        w1_raw0 = load_weight("w1a", w1[0:512, :], 1)
        w1_raw1 = load_weight("w1b", w1[512:1024, :], 2)
        nc.sync.dma_start(out=w2_w[:].bitcast(I32), in_=w2_words.rearrange("a p c -> p a c").bitcast(I32))
        load_scales(w2_s, w2_scales)
        load_words(tab_w[1], tab_words[1])
        w3_raw = load_weight("w3", w3, 1)
        nc.sync.dma_start(out=gain_t[:], in_=gain.rearrange("(p t) -> p t", t=PACK))
        load_wgs(0)
        load_page(0)
        load_words(tab2_w, tab2_words[0])
        load_page(1)
        load_page(2)
        load_page(3)
        load_wgs(1)
        load_wgs(2)
        load_wgs(3)
        nc.sync.dma_start(out=tune_t[:], in_=tune.rearrange("(p t) -> p t", t=PACK))
        with nc.allow_non_contiguous_dma(reason="one least score a partition"):
            nc.sync.dma_start(out=least_t[:], in_=least.rearrange("(c p) -> p c", p=P))

        def quantise_weight(name, raws, dealt=False):
            grouped = held(f"{name}_g", [P, H, PACK], BF16)
            codes = held(f"{name}_c", [P, H], U32)
            plane = held(f"{name}_s", [P, H], U8)
            width = H // len(raws)
            for c, raw in enumerate(raws):
                if dealt:
                    rows = slice(c * width // PACK, (c + 1) * width // PACK)
                    target = grouped[:].rearrange("p (t m) j -> p m j t", t=PACK)[:, rows, :, :]
                else:
                    target = grouped[:, c * width:(c + 1) * width, :].rearrange("p (m t) j -> p m j t", t=PACK)
                nc.scalar.copy(out=target, in_=raw.rearrange("p j (m t) -> p m j t", t=PACK))
            nc.vector.quantize_mx(out=codes[:].bitcast(FP8X4), scales=plane[:], in_=grouped[:].rearrange("p c j -> p (c j)"))
            return codes, plane

        for a in range(PASSES):
            nc.vector.tensor_copy(v_s[a][:], tab_s[:, a, :].indirect(idx[:]))
        nc.vector.tensor_copy(v_w[0][:], tab_w[0][:].bitcast(U32).indirect(idx[:]))
        make_identity(nc, ident[:])
        w1_q = [quantise_weight("w1a", w1_raw0)]
        nc.vector.tensor_copy(v2_s[:], tab2_s[:, 0, :].indirect(idx2[:]))
        w1_q.append(quantise_weight("w1b", w1_raw1))
        for u in range(2):
            nc.vector.tensor_copy(v_w[1][:, u * S // 2:(u + 1) * S // 2], tab_w[1][:].bitcast(U32).indirect(idx[:, u * S // 32:(u + 1) * S // 32]))
        w3_c, w3_s = quantise_weight("w3", w3_raw, True)

        def bank(tag, bufs, shape):
            return psum.tile(shape, F32, name=tag, tag=tag, bufs=bufs)

        def front(c):
            cols = slice(c * CHUNK, (c + 1) * CHUNK)
            a_ps = bank("a", 2, [P, H])
            b_ps = bank("b", 2, [P, H])
            for a in range(PASSES):
                nc.tensor.matmul_mx(out=a_ps[:], lhsT=v_w[a][:, cols].bitcast(FP8X4), lhsT_scale=v_s[a][:, cols],
                                    rhs=w1_q[a][0][:].bitcast(FP8X4), rhs_scale=w1_q[a][1][:],
                                    start=(a == 0), stop=(a == PASSES - 1))
            for a in range(PASSES):
                nc.tensor.matmul_mx(out=b_ps[:], lhsT=v_w[a][:, cols].bitcast(FP8X4), lhsT_scale=v_s[a][:, cols],
                                    rhs=w2_w[:, a, :].bitcast(FP4X4), rhs_scale=w2_s[:, a, :],
                                    start=(a == 0), stop=(a == PASSES - 1))
            a_sb = held(f"a_sb{c}", [P, PACK, P], F32)
            nc.scalar.copy(out=a_sb[:], in_=a_ps[:].rearrange("p (m t) -> p t m", t=PACK))
            d_t = ring.tile([P, 2, P, 2], BF16, name="d_t")
            nc.vector.tensor_tensor(d_t[:], b_ps[:].rearrange("p (m u e) -> p u m e", u=2, e=2),
                                    a_sb[:].rearrange("p (u e) m -> p u m e", e=2), ALU.max)
            d_words = d_t[:].rearrange("p u m e -> p (u m e)").bitcast(F32)
            d_ps = bank("d", 1, [P, 2, CHUNK])
            for u in range(2):
                nc.tensor.transpose(d_ps[:, u, :], d_words[:, u * P:(u + 1) * P], ident[:])
            d_g = ring.tile([P, CHUNK * PACK], BF16, name="d_g", align_bytes=64)
            nc.scalar.copy(out=d_g[:].bitcast(F32).rearrange("p (j u) -> p j u", u=2), in_=d_ps[:].rearrange("p u j -> p j u"))
            d_c = held(f"d_c{c}", [P, CHUNK], U32)
            d_s = held(f"d_s{c}", [P, CHUNK], U8)
            nc.vector.quantize_mx(out=d_c[:].bitcast(FP8X4), scales=d_s[:], in_=d_g[:])
            return a_sb, d_c, d_s

        def back(c, h_tiles, a_sb, d_c, d_s):
            at = (c * CHUNK) % SLICE
            h_ps = bank("h", 2, [P, PACK, CHUNK])
            if c < SLICE // CHUNK:
                for t in range(PACK):
                    nc.tensor.transpose(h_ps[:, t, :], a_sb[:, t, :], ident[:])
                a_gain = ring.tile([P, PACK, CHUNK], F32, name="a_gain")
                for t in range(PACK):
                    nc.scalar.activation(a_gain[:, t, :], h_ps[:, t, :], COPY, scale=gain_t[:, t:t + 1])
                y_ps = bank("y", 1, [P, PACK, CHUNK])
                for t in range(PACK):
                    nc.tensor.matmul_mx(out=y_ps[:, t, :], lhsT=w3_c[:, t * P:(t + 1) * P].bitcast(FP8X4), lhsT_scale=w3_s[:, t * P:(t + 1) * P],
                                        rhs=d_c[:].bitcast(FP8X4), rhs_scale=d_s[:], start=True, stop=True)
                for t in range(PACK):
                    nc.vector.scalar_tensor_tensor(h_tiles[t][:, at:at + CHUNK], y_ps[:, t, :], gain_t[:, t:t + 1], a_gain[:, t, :],
                                                   ALU.mult, ALU.add)
                return
            y_ps = bank("y", 1, [P, H])
            nc.tensor.matmul_mx(out=y_ps[:], lhsT=d_c[:].bitcast(FP8X4), lhsT_scale=d_s[:],
                                rhs=w3_c[:].bitcast(FP8X4), rhs_scale=w3_s[:], start=True, stop=True)
            y_sb = ring.tile([P, H], F32, name="y_sb")
            nc.scalar.copy(out=y_sb[:], in_=y_ps[:])
            for t in range(PACK):
                nc.tensor.matmul(h_ps[:, t, :], lhsT=a_sb[:, t, :], rhs=ident[:], is_transpose=True, start=True, stop=False)
                nc.tensor.matmul(h_ps[:, t, :], lhsT=y_sb[:, t * P:(t + 1) * P], rhs=ident[:], is_transpose=True, start=False, stop=True)
            for t in range(PACK):
                nc.scalar.activation(h_tiles[t][:, at:at + CHUNK], h_ps[:, t, :], COPY, scale=gain_t[:, t:t + 1])

        x_g = [held(f"x_g{u}", [P, HALF, PACK], BF16) for u in range(2)]

        def fetch(t, u):
            picked = held(f"picked{t}_{u}", [P, HALF], F32)
            nc.vector.tensor_copy(picked[:], page[t][:].indirect(idx4[:, u * (HALF // 16):(u + 1) * (HALF // 16)]))
            nc.scalar.activation(x_g[u][:, :, t], picked[:], COPY, scale=tune_t[:, t:t + 1])

        per = SLICE // CHUNK
        fronts = {}
        h_all = [[held(f"h{s}_{t}", [P, SLICE], F32) for t in range(PACK)] for s in range(N_SLICES)]

        def fronts_of(s):
            for c in range(s * per, (s + 1) * per):
                fronts[c] = front(c)

        def backs_of(s):
            for c in range(s * per, (s + 1) * per):
                back(c, h_all[s], *fronts[c])

        fronts_of(0)
        backs_of(0)
        fronts_of(1)
        nc.vector.tensor_copy(v2_w[:], tab2_w[:].bitcast(U32).indirect(idx2[:]))
        for s in range(N_SLICES):
            h_tiles = h_all[s]
            if s + 2 < N_SLICES:
                fronts_of(s + 2)
            for t in range(PACK):
                if s == N_SLICES - 1 and t == PACK - 1:
                    for done in range(1, PACK - 1):
                        fetch(done, 0)
                        fetch(done, 1)
                nc.vector.tensor_tensor(page[t][:].indirect(idx3[:, s * (SLICE // 16):(s + 1) * (SLICE // 16)]),
                                        h_tiles[t][:], wgs_t[s][:, t, :], ALU.mult)
                if s == N_SLICES - 1 and t in (0, PACK - 1):
                    fetch(t, 0)
                    fetch(t, 1)
            if s + 1 < N_SLICES:
                backs_of(s + 1)

        tags = [("a", 2), ("a", 2), ("b", 2), ("b", 2), ("h", 2), ("h", 2), ("d", 1), ("y", 1)]
        out_rows = out.rearrange("(c p) j -> p c j", p=P)
        for u in range(2):
            x_c = held(f"x_c{u}", [P, HALF], U32)
            x_s = held(f"x_s{u}", [P, HALF], U8)
            nc.vector.quantize_mx(out=x_c[:].bitcast(FP8X4), scales=x_s[:], in_=x_g[u][:].rearrange("p j t -> p (j t)"))
            for pair in range(CAND // P // 2):
                tag, bufs = tags[u * 4 + pair]
                e_ps = bank(tag, bufs, [P, 2, HALF])
                for i in range(2):
                    cols = slice((2 * pair + i) * P, (2 * pair + i + 1) * P)
                    nc.tensor.matmul_mx(out=e_ps[:, i, :], lhsT=v2_w[:, cols].bitcast(FP8X4), lhsT_scale=v2_s[:, cols],
                                        rhs=x_c[:].bitcast(FP8X4), rhs_scale=x_s[:], start=True, stop=True)
                scores = held(f"scores{u}_{pair}", [P, 2, HALF], F32)
                nc.vector.tensor_tensor(scores[:], e_ps[:],
                                        least_t[:, 2 * pair:2 * pair + 2].unsqueeze(2).to_broadcast([P, 2, HALF]), ALU.max)
                nc.sync.dma_start(out=out_rows[:, 2 * pair:2 * pair + 2, u * HALF:(u + 1) * HALF], in_=scores[:])
